import numpy as np
import ml_dtypes


def mxq(x, axis, fmt="e4m3"):
    dtype, down = {"e4m3": (ml_dtypes.float8_e4m3fn, 7), "e5m2": (ml_dtypes.float8_e5m2, 14)}[fmt]
    v = np.moveaxis(np.asarray(x, np.float32).astype(ml_dtypes.bfloat16).astype(np.float64), axis, -1)
    blocks = v.reshape(v.shape[:-1] + (-1, 32))
    amax = np.abs(blocks).max(-1, keepdims=True)
    byte = np.maximum(np.where(amax > 0, np.frexp(amax)[1] - 1 + 127, 0) - down, 1)
    scale = np.exp2(byte - 127.0)
    codes = (blocks / scale).astype(np.float32).astype(dtype).astype(np.float64)
    return np.moveaxis((codes * scale).reshape(v.shape), -1, axis)


WIDE = False


def mx_kscale(k):
    if not WIDE:
        return np.ones(k)
    levels = np.array([10, -10, 5, -5, 0])
    if k % 512:
        return np.exp2(np.random.permutation(np.resize(levels, k // 32))).repeat(32)
    a = np.empty((k // 512, 16))
    for p in range(k // 512):
        a[p, :8] = np.random.permutation(np.resize(levels, 8))
        for g in range(8):
            far = levels[np.abs(levels - a[p, g]) >= 10]
            a[p, g + 8] = far[np.random.randint(len(far))]
    return np.exp2(a.ravel()).repeat(32)


def f64(x):
    return np.asarray(x).astype(np.float64)


def striped(idx):
    return np.tile(idx.reshape(-1, 16).T, (8, 1)).astype(np.uint16)


def unstriped(offs):
    return offs[:16].T.reshape(-1).astype(np.int64)


E2M1 = np.array([0.0, 0.5, 1.0, 1.5, 2.0, 3.0, 4.0, 6.0, -0.0, -0.5, -1.0, -1.5, -2.0, -3.0, -4.0, -6.0])


def pack_weight(w, fmt):
    k, n = w.shape
    w = f64(np.asarray(w, np.float32).astype(ml_dtypes.bfloat16)).reshape(k // 32, 32, n)
    amax = np.abs(w).max(1)
    if fmt == "e4m3":
        byte = np.frexp(amax)[1] - 1 + 127 - 7
    else:
        mant, ex = np.frexp(amax / 6.0)
        byte = np.where(mant > 0.5, ex, ex - 1) + 127
    byte = np.clip(np.where(amax > 0, byte, 1), 1, 254)
    scaled = (w * np.exp2(127.0 - byte)[:, None, :]).reshape(k, n).astype(np.float32)
    by_word = np.ascontiguousarray(scaled.reshape(k // 512, 128, 4, n).transpose(0, 1, 3, 2))
    if fmt == "e4m3":
        words = by_word.astype(ml_dtypes.float8_e4m3fn).view(np.uint8)
    else:
        c = by_word.astype(ml_dtypes.float4_e2m1fn).view(np.uint8) & 0xF
        words = (c[..., 0::2] | (c[..., 1::2] << 4)).reshape(k // 512, 128, 2 * n)
    return np.ascontiguousarray(words), np.ascontiguousarray(byte.astype(np.uint8).reshape(k // 512, 16, n))


def unpack_weight(words, scales, fmt):
    g, _, n = scales.shape
    words = np.ascontiguousarray(words).reshape(g, 128, n, -1)
    if fmt == "e4m3":
        vals = words.view(ml_dtypes.float8_e4m3fn).astype(np.float64)
    else:
        nib = np.empty((g, 128, n, 4), np.uint8)
        nib[..., 0::2] = words & 0xF
        nib[..., 1::2] = words >> 4
        vals = E2M1[nib]
    vals = vals * np.repeat(np.exp2(scales.astype(np.float64) - 127.0), 8, axis=1)[..., None]
    return vals.transpose(0, 1, 3, 2).reshape(g * 512, n)


def gelu(v):
    return 0.5 * v * (1.0 + np.tanh(np.sqrt(2.0 / np.pi) * (v + 0.044715 * v**3)))


K, T, S, H, P = 1024, 4096, 1024, 1024, 512

def setup_inputs():
    n = np.random.standard_normal
    s = mx_kscale(K)[:, None]
    u = mx_kscale(H)[:, None]
    tab_words, tab_scales = pack_weight(n((K, T)) * s, "e4m3")
    w1 = n((K, H)) / np.sqrt(K) / s * u.T
    w4_words, w4_scales = pack_weight(0.52 * n((K, H)) / np.sqrt(K) / s, "e2m1")
    b1 = 0.6 * n(H) * u[:, 0]
    gain = 3.0 * np.exp(0.4 * n(H)) / np.sqrt(H) / u[:, 0] ** 2
    client = np.exp(0.4 * n((P, P)))
    d = 0.5 * n(P)
    return {"tab_words": tab_words, "tab_scales": tab_scales,
            "offs": striped(np.random.permutation(T)[:S]),
            "pos1": striped(np.random.permutation(S)[:P]),
            "pos2": striped(np.random.permutation(S)[:P]),
            "w1": w1.astype(np.float32), "b1": b1.astype(np.float32),
            "w4_words": w4_words, "w4_scales": w4_scales,
            "gain": gain.astype(np.float32),
            "client": client.astype(np.float32), "d": d.astype(np.float32)}

def reference(tab_words, tab_scales, offs, pos1, pos2, w1, b1, w4_words, w4_scales, gain, client, d):
    v = unpack_weight(tab_words, tab_scales, "e4m3")[:, unstriped(offs)]
    w4 = unpack_weight(w4_words, w4_scales, "e2m1")
    a = mxq(f64(w1), 0, "e4m3").T @ v
    b = w4.T @ v
    h = (a + f64(b1)[:, None]) * np.sin(b)
    x1 = h[:, unstriped(pos1)]
    x2 = np.abs(h[:, unstriped(pos2)]) * f64(gain)[:, None]
    e = mxq(x1, 0, "e4m3").T @ mxq(x2, 0, "e4m3")
    return e * f64(client) + f64(d)[:, None]

@@ -1,0 +1,279 @@
+from contextlib import ExitStack
+import math
+
+import concourse.mybir as mybir
+from concourse.masks import make_identity
+
+K, T, S, H, NP = 1024, 4096, 1024, 1024, 512
+FLOPS = 2 * (2 * K * H * S + H * NP * NP)
+
+F32 = mybir.dt.float32
+BF16 = mybir.dt.bfloat16
+I32 = mybir.dt.int32
+U32 = mybir.dt.uint32
+U16 = mybir.dt.uint16
+U8 = mybir.dt.uint8
+FP8X4 = mybir.dt.float8_e4m3fn_x4
+FP4X4 = mybir.dt.float4_e2m1fn_x4
+ALU = mybir.AluOpType
+ACT = mybir.ActivationFunctionType
+
+P = 128
+BANK = 512
+PASSES = 2
+TILES = 8
+TURN = 2.0 * math.pi
+WHOLE = 1.5 * 2.0**23
+VECTOR_TILES = 2
+
+
+def tile_list_segment_redundancy_scores_kernel(
+    tc, tab_words, tab_scales, offs, pos1, pos2, w1, b1, w4_words, w4_scales, gain, client, d, out
+):
+    nc = tc.nc
+    with ExitStack() as ctx:
+        lists = ctx.enter_context(tc.tile_pool(name="lists", bufs=1))
+        keep = ctx.enter_context(tc.tile_pool(name="keep", bufs=1))
+        ring = ctx.enter_context(tc.tile_pool(name="ring", bufs=3))
+        big = ctx.enter_context(tc.tile_pool(name="big", bufs=1))
+        psum = ctx.enter_context(tc.psum_pool(name="psum", bufs=4))
+
+        tab_sc = keep.tile([P, T], U8, name="tab_sc")
+        w4_sc_raw = keep.tile([P, PASSES, H], U8, name="w4_sc_raw")
+        rows = keep.tile([P, P], F32, name="rows")
+        nc.vector.memset(tab_sc[:].bitcast(I32), 0)
+        nc.gpsimd.memset(w4_sc_raw[:].rearrange("p a c -> p (a c)").bitcast(I32), 0)
+        nc.vector.memset(rows[:], 0.0)
+        v_sc1 = keep.tile([P, S], U8, name="v_sc1", align_bytes=64)
+        nc.gpsimd.memset(v_sc1[:].bitcast(I32), 0)
+
+        offs_t = lists.tile([P, S // 16], U16, name="offs_t")
+        pos1_t = lists.tile([P, NP // 16], U16, name="pos1_t")
+        pos2_t = lists.tile([P, NP // 16], U16, name="pos2_t")
+        nc.sync.dma_start(offs_t[:], offs)
+        nc.sync.dma_start(pos2_t[:], pos2)
+        nc.sync.dma_start(pos1_t[:], pos1)
+        tab_w = [big.tile([P, T], I32, name="tab_w%d" % a, offset=4 * T * a) for a in range(PASSES)]
+        w4_raw = keep.tile([P, PASSES, H // 2], I32, name="w4_raw", tag="w4_raw")
+        for q in range(4):
+            nc.sync.dma_start(tab_sc[32 * q : 32 * q + 8, :].bitcast(I32), tab_scales[:, 4 * q : 4 * q + 4, :].bitcast(I32))
+        nc.sync.dma_start(tab_w[0][:], tab_words[0].rearrange("p t i -> p (t i)").bitcast(I32))
+        for q in range(4):
+            nc.sync.dma_start(
+                w4_sc_raw[32 * q : 32 * q + 4, :, :].bitcast(I32),
+                w4_scales[:, 4 * q : 4 * q + 4, :].rearrange("a q c -> q a c").bitcast(I32),
+            )
+        nc.sync.dma_start(w4_raw[:], w4_words.rearrange("a p c -> p a c").bitcast(I32))
+        nc.sync.dma_start(tab_w[1][:], tab_words[1].rearrange("p t i -> p (t i)").bitcast(I32))
+        for first, vec in ((TILES, gain), (0, b1)):
+            for b in range(2):
+                nc.sync.dma_start(
+                    rows[first + 4 * b : first + 4 * b + 4, :].rearrange("t (g q) -> t g q", q=8),
+                    vec[512 * b : 512 * (b + 1)].rearrange("(g t q) -> t g q", t=4, q=8),
+                )
+        nc.sync.dma_start(rows[2 * TILES : 2 * TILES + 4, :], d.rearrange("(u p) -> u p", p=P))
+
+        v_sc = keep.tile([P, S], U8, name="v_sc", align_bytes=64)
+        nc.vector.tensor_copy(v_sc[:], tab_sc[:].indirect(offs_t[:]))
+        nc.scalar.dma_start(v_sc1[0:112, :].bitcast(I32), v_sc[4:116, :].bitcast(I32))
+        v_planes = (v_sc, v_sc1)
+        v_w = {}
+
+        def gather_words(a):
+            for half in range(2):
+                words = keep.tile([P, BANK], U32, name="v_w%d%d" % (a, half), align_bytes=64)
+                nc.vector.tensor_copy(words[:], tab_w[a][:].bitcast(U32).indirect(offs_t[:, 32 * half : 32 * (half + 1)]))
+                v_w[a, half] = words
+
+        gather_words(0)
+        w4_w = keep.tile([P, PASSES * TILES * 2 * P], U8, name="w4_w", align_bytes=64)
+        w4_sc = keep.tile([P, PASSES * TILES * P], U8, name="w4_sc", align_bytes=64)
+        nc.vector.tensor_copy(
+            w4_w[:].bitcast(I32).rearrange("p (n t g w) -> p n t g w", t=4, g=16, w=4),
+            w4_raw[:].rearrange("p a c -> p (a c)").rearrange("p (n g t w) -> p n t g w", t=4, g=16, w=4),
+        )
+        nc.vector.tensor_copy(
+            w4_sc[:].bitcast(I32).rearrange("p (n t g w) -> p n t g w", t=4, g=16, w=2),
+            w4_sc_raw[:].rearrange("p a c -> p (a c)").bitcast(I32).rearrange("p (n g t w) -> p n t g w", t=4, g=16, w=2),
+        )
+        gather_words(1)
+
+        w1_raw = {}
+        for b in range(2):
+            for a in range(PASSES):
+                raw = big.tile([P, 4, 512], F32, name="w1_raw%d%d" % (a, b), offset=4 * T * b + 2 * T * a)
+                nc.sync.dma_start(
+                    raw[:], w1[512 * a : 512 * (a + 1), 512 * b : 512 * (b + 1)].rearrange("(p j) c -> p j c", j=4)
+                )
+                w1_raw[a, b] = raw
+        client_t = keep.tile([P, 4, NP], F32, name="client_t", tag="w4_raw")
+        nc.sync.dma_start(client_t[:], client.rearrange("(u p) j -> p u j", p=P))
+
+        ident = keep.tile([P, P], F32, name="ident")
+        make_identity(nc, ident[:])
+        turned = psum.tile([P, P], F32, name="turned", tag="a")
+        nc.tensor.transpose(turned[:], rows[:], ident[:])
+        cols = keep.tile([P, 2 * TILES + 4], F32, name="cols")
+        nc.vector.tensor_copy(cols[:], turned[:, 0 : 2 * TILES + 4])
+        positive = keep.tile([P, TILES], F32, name="positive")
+        nc.vector.tensor_scalar(positive[:], cols[:, TILES : 2 * TILES], 0.0, 2.0 * TURN, ALU.is_ge, ALU.mult)
+        signed_turn = keep.tile([P, TILES], F32, name="signed_turn")
+        nc.vector.tensor_scalar(signed_turn[:], positive[:], 1.0, -TURN, ALU.mult, ALU.add)
+
+        fracs = {}
+        picked = {}
+        sines = {}
+        w1_q = {}
+
+        def reduce_b(n):
+            frac = ring.tile([P, S], F32, name="frac")
+            by_vector = n < VECTOR_TILES
+            if not by_vector:
+                turns = ring.tile([P, S], F32, name="turns")
+            whole = ring.tile([P, S], I32, name="whole")
+            for half in range(2):
+                cs = slice(BANK * half, BANK * (half + 1))
+                acc = psum.tile([P, BANK], F32, name="acc_b", tag="b")
+                for a in range(PASSES):
+                    at = a * TILES + n
+                    nc.tensor.matmul_mx(
+                        out=acc[:],
+                        lhsT=w4_w[:, 2 * P * at : 2 * P * (at + 1)].bitcast(FP4X4),
+                        lhsT_scale=w4_sc[:, P * at : P * (at + 1)],
+                        rhs=v_w[a, half][:].bitcast(FP8X4),
+                        rhs_scale=v_planes[a][:, cs],
+                        start=(a == 0),
+                        stop=(a == PASSES - 1),
+                    )
+                if by_vector:
+                    nc.vector.tensor_scalar(whole[:, cs], acc[:], 1.0 / TURN, None, ALU.mult)
+                    nc.vector.scalar_tensor_tensor(frac[:, cs], acc[:], 1.0 / TURN, whole[:, cs], ALU.mult, ALU.subtract)
+                else:
+                    nc.scalar.activation(turns[:, cs], acc[:], ACT.Copy, scale=-1.0 / TURN)
+            if not by_vector:
+                nc.scalar.activation(whole[:].bitcast(U32), turns[:], ACT.Copy, bias=WHOLE)
+                nc.vector.scalar_tensor_tensor(frac[:], whole[:], WHOLE, turns[:], ALU.subtract, ALU.subtract)
+            fracs[n] = frac
+
+        def sine_of_b(n):
+            sine = ring.tile([P, S], F32, name="sine", bufs=3)
+            nc.scalar.activation(sine[:], fracs[n][:], ACT.Sin, scale=signed_turn[:, n : n + 1])
+            sines[n] = sine
+
+        def quantise_w1(n):
+            b, t = divmod(n, 4)
+            grouped = ring.tile([P, PASSES, 4 * P], BF16, name="grouped", align_bytes=64)
+            for a in range(PASSES):
+                nc.scalar.copy(
+                    grouped[:, a, :].rearrange("p (g h i j) -> p g h j i", h=2, i=4, j=4),
+                    w1_raw[a, b][:].rearrange("p j (g t h i) -> p t g h j i", t=4, h=2, i=4)[:, t],
+                )
+            codes = keep.tile([P, PASSES * P], U32, name="w1_codes%d" % n, align_bytes=64)
+            scales = keep.tile([P, PASSES * P], U8, name="w1_scales%d" % n, align_bytes=64)
+            nc.vector.quantize_mx(out=codes[:].bitcast(FP8X4), scales=scales[:], in_=grouped[:].rearrange("p a c -> p (a c)"))
+            w1_q[n] = (codes, scales)
+
+        planes1 = [keep.tile([P, 4, NP], BF16, name="planes1_%d" % b) for b in range(2)]
+        planes2 = [keep.tile([P, 4, NP], BF16, name="planes2_%d" % b) for b in range(2)]
+
+        def rows_of_h(n):
+            b, t = divmod(n, 4)
+            codes, scales = w1_q[n]
+            h = ring.tile([P, S], F32, name="h")
+            for half in range(2):
+                cs = slice(BANK * half, BANK * (half + 1))
+                acc = psum.tile([P, BANK], F32, name="acc_a", tag="a")
+                for a in range(PASSES):
+                    nc.tensor.matmul_mx(
+                        out=acc[:],
+                        lhsT=codes[:, P * a : P * (a + 1)].bitcast(FP8X4),
+                        lhsT_scale=scales[:, P * a : P * (a + 1)],
+                        rhs=v_w[a, half][:].bitcast(FP8X4),
+                        rhs_scale=v_planes[a][:, cs],
+                        start=(a == 0),
+                        stop=(a == PASSES - 1),
+                    )
+                nc.vector.scalar_tensor_tensor(h[:, cs], acc[:], cols[:, n : n + 1], sines[n][:, cs], ALU.add, ALU.mult)
+            picked2 = ring.tile([P, NP], F32, name="picked2")
+            nc.vector.tensor_copy(picked2[:], h[:].indirect(pos2_t[:]))
+            nc.vector.tensor_copy(planes1[b][:, t, :], h[:].indirect(pos1_t[:]))
+            picked[n] = picked2
+
+        def magnitude(n):
+            b, t = divmod(n, 4)
+            nc.scalar.activation(planes2[b][:, t, :], picked[n][:], ACT.Abs, scale=cols[:, TILES + n : TILES + n + 1])
+
+        woven = {}
+        x_q = {}
+        for which in (1, 2):
+            for b in range(2):
+                woven[which, b] = keep.tile([P, NP, 4], BF16, name="woven%d_%d" % (which, b), align_bytes=64)
+                x_q[which, b] = (
+                    keep.tile([P, NP], U32, name="x_codes%d_%d" % (which, b), align_bytes=64),
+                    keep.tile([P, NP], U8, name="x_scales%d_%d" % (which, b), align_bytes=64),
+                )
+        planes = {1: planes1, 2: planes2}
+
+        def weave(copy, which, b, lo, hi):
+            copy(
+                woven[which, b][:, lo:hi, :].rearrange("p (c i) t -> p c t i", i=4),
+                planes[which][b][:, :, lo:hi].rearrange("p t (c i) -> p c t i", i=4),
+            )
+
+        def quantise_x(which, b, lo, hi):
+            codes, scales = x_q[which, b]
+            nc.vector.quantize_mx(
+                out=codes[:, lo:hi].bitcast(FP8X4),
+                scales=scales[:, lo:hi],
+                in_=woven[which, b][:, lo:hi, :].rearrange("p c t -> p (c t)"),
+            )
+
+        scores = []
+
+        def score_pass(u, b):
+            if b == 0:
+                scores.append(psum.tile([P, NP], F32, name="acc_e", tag="b"))
+            nc.tensor.matmul_mx(
+                out=scores[u][:],
+                lhsT=x_q[1, b][0][:, P * u : P * (u + 1)].bitcast(FP8X4),
+                lhsT_scale=x_q[1, b][1][:, P * u : P * (u + 1)],
+                rhs=x_q[2, b][0][:].bitcast(FP8X4),
+                rhs_scale=x_q[2, b][1][:],
+                start=(b == 0),
+                stop=(b == 1),
+            )
+
+        def finish(u):
+            score_pass(u, 1)
+            weighted = ring.tile([P, NP], F32, name="weighted", bufs=4)
+            nc.vector.tensor_tensor(weighted[:], scores[u][:], client_t[:, u, :], ALU.mult)
+            scored = ring.tile([P, NP], F32, name="scored", bufs=4)
+            nc.scalar.activation(scored[:], weighted[:], ACT.Identity, bias=cols[:, 2 * TILES + u : 2 * TILES + u + 1])
+            nc.sync.dma_start(out[P * u : P * (u + 1), :], scored[:])
+
+        for n in range(-2, TILES + 1):
+            if n + 2 < TILES:
+                quantise_w1(n + 2)
+                reduce_b(n + 2)
+            if 0 <= n + 1 < TILES:
+                sine_of_b(n + 1)
+            if 0 <= n < TILES:
+                rows_of_h(n)
+            if 0 <= n - 1:
+                magnitude(n - 1)
+            if n in (5, 6):
+                which = 2 if n == 5 else 1
+                weave(nc.scalar.copy, which, 0, 0, 256)
+                weave(nc.scalar.copy, which, 0, 256, 512)
+                quantise_x(which, 0, 0, NP)
+            if n == 7:
+                for u in range(4):
+                    score_pass(u, 0)
+        weave(nc.scalar.copy, 2, 1, 0, 192)
+        weave(nc.vector.tensor_copy, 2, 1, 192, NP)
+        quantise_x(2, 1, 0, NP)
+        for half in range(2):
+            weave(nc.scalar.copy, 1, 1, 256 * half, 256 * (half + 1))
+            quantise_x(1, 1, 256 * half, 256 * (half + 1))
+            finish(2 * half)
+            finish(2 * half + 1)

@@ -22,9 +22,11 @@ P = 128
 BANK = 512
 PASSES = 2
 TILES = 8
+KIB = 1024
+W1_AT = {(0, 0): 10, (1, 0): 2, (0, 1): 24, (1, 1): 32}
 TURN = 2.0 * math.pi
 WHOLE = 1.5 * 2.0**23
-VECTOR_TILES = 2
+VECTOR_TILES = (0, 1, 2)
 
 
 def tile_list_segment_redundancy_scores_kernel(
@@ -38,87 +40,98 @@ def tile_list_segment_redundancy_scores_kernel(
         big = ctx.enter_context(tc.tile_pool(name="big", bufs=1))
         psum = ctx.enter_context(tc.psum_pool(name="psum", bufs=4))
 
-        tab_sc = keep.tile([P, T], U8, name="tab_sc")
-        w4_sc_raw = keep.tile([P, PASSES, H], U8, name="w4_sc_raw")
-        rows = keep.tile([P, P], F32, name="rows")
+        tab_sc = keep.tile([P, T], U8, name="tab_sc", tag="picked01", align_bytes=64)
+        rows = keep.tile([P, 512], F32, name="rows", tag="picked00", align_bytes=64)
+        tab_sc_rows = keep.tile([P, T // 4], I32, name="tab_sc_rows")
+        w4_sc_raw = keep.tile([P, PASSES, H], U8, name="w4_sc_raw", tag="picked11", align_bytes=64)
+        dealt = keep.tile([P, 4, P], F32, name="dealt")
         nc.vector.memset(tab_sc[:].bitcast(I32), 0)
-        nc.gpsimd.memset(w4_sc_raw[:].rearrange("p a c -> p (a c)").bitcast(I32), 0)
-        nc.vector.memset(rows[:], 0.0)
+        nc.gpsimd.memset(dealt[:], 0.0)
         v_sc1 = keep.tile([P, S], U8, name="v_sc1", align_bytes=64)
         nc.gpsimd.memset(v_sc1[:].bitcast(I32), 0)
 
         offs_t = lists.tile([P, S // 16], U16, name="offs_t")
         pos1_t = lists.tile([P, NP // 16], U16, name="pos1_t")
         pos2_t = lists.tile([P, NP // 16], U16, name="pos2_t")
+        tab_w = [big.tile([P, T], I32, name="tab_w%d" % a, offset=(8 + 16 * a) * KIB) for a in range(PASSES)]
+        w4_raw = keep.tile([P, PASSES, H // 2], I32, name="w4_raw", tag="picked10", align_bytes=64)
         nc.sync.dma_start(offs_t[:], offs)
-        nc.sync.dma_start(pos2_t[:], pos2)
-        nc.sync.dma_start(pos1_t[:], pos1)
-        tab_w = [big.tile([P, T], I32, name="tab_w%d" % a, offset=4 * T * a) for a in range(PASSES)]
-        w4_raw = keep.tile([P, PASSES, H // 2], I32, name="w4_raw", tag="w4_raw")
         for q in range(4):
-            nc.sync.dma_start(tab_sc[32 * q : 32 * q + 8, :].bitcast(I32), tab_scales[:, 4 * q : 4 * q + 4, :].bitcast(I32))
+            nc.sync.dma_start(tab_sc_rows[32 * q : 32 * q + 8, :], tab_scales[:, 4 * q : 4 * q + 4, :].bitcast(I32))
+        nc.sync.dma_start(rows[0:2, :], b1.rearrange("(b c) -> b c", b=2))
+        nc.sync.dma_start(rows[2:4, :], gain.rearrange("(b c) -> b c", b=2))
         nc.sync.dma_start(tab_w[0][:], tab_words[0].rearrange("p t i -> p (t i)").bitcast(I32))
+        nc.sync.dma_start(w4_raw[:], w4_words.rearrange("a p c -> p a c").bitcast(I32))
         for q in range(4):
             nc.sync.dma_start(
                 w4_sc_raw[32 * q : 32 * q + 4, :, :].bitcast(I32),
                 w4_scales[:, 4 * q : 4 * q + 4, :].rearrange("a q c -> q a c").bitcast(I32),
             )
-        nc.sync.dma_start(w4_raw[:], w4_words.rearrange("a p c -> p a c").bitcast(I32))
         nc.sync.dma_start(tab_w[1][:], tab_words[1].rearrange("p t i -> p (t i)").bitcast(I32))
-        for first, vec in ((TILES, gain), (0, b1)):
-            for b in range(2):
-                nc.sync.dma_start(
-                    rows[first + 4 * b : first + 4 * b + 4, :].rearrange("t (g q) -> t g q", q=8),
-                    vec[512 * b : 512 * (b + 1)].rearrange("(g t q) -> t g q", t=4, q=8),
-                )
-        nc.sync.dma_start(rows[2 * TILES : 2 * TILES + 4, :], d.rearrange("(u p) -> u p", p=P))
+        nc.sync.dma_start(pos2_t[:], pos2)
+        nc.sync.dma_start(pos1_t[:], pos1)
+
+        for q in range(4):
+            nc.vector.tensor_copy(tab_sc[32 * q : 32 * q + 8, :].bitcast(I32), tab_sc_rows[32 * q : 32 * q + 8, :])
+
+        v_w = {}
+
+        def gather_words(a):
+            for half in range(2):
+                words = keep.tile([P, BANK], U32, name="v_w%d%d" % (a, half), tag="picked%d%d" % (a, half), align_bytes=64)
+                nc.vector.tensor_copy(words[:], tab_w[a][:].bitcast(U32).indirect(offs_t[:, 32 * half : 32 * (half + 1)]))
+                v_w[a, half] = words
 
         v_sc = keep.tile([P, S], U8, name="v_sc", align_bytes=64)
         nc.vector.tensor_copy(v_sc[:], tab_sc[:].indirect(offs_t[:]))
         nc.scalar.dma_start(v_sc1[0:112, :].bitcast(I32), v_sc[4:116, :].bitcast(I32))
         v_planes = (v_sc, v_sc1)
-        v_w = {}
-
-        def gather_words(a):
-            for half in range(2):
-                words = keep.tile([P, BANK], U32, name="v_w%d%d" % (a, half), align_bytes=64)
-                nc.vector.tensor_copy(words[:], tab_w[a][:].bitcast(U32).indirect(offs_t[:, 32 * half : 32 * (half + 1)]))
-                v_w[a, half] = words
+        ident = keep.tile([P, P], F32, name="ident")
+        make_identity(nc, ident[:])
+        nc.vector.tensor_copy(
+            dealt[0:4].rearrange("p t (g q) -> p t g q", q=8), rows[0:4, :].rearrange("p (g t q) -> p t g q", t=4, q=8)
+        )
+        turned = psum.tile([P, 4, P], F32, name="turned", tag="a")
+        for t in range(4):
+            nc.tensor.transpose(turned[:, t, :], dealt[:, t, :], ident[:])
+        cols = keep.tile([P, 2 * TILES], F32, name="cols")
+        nc.vector.tensor_copy(cols[:].rearrange("p (n t) -> p n t", t=4), turned[:, :, 0:4].rearrange("p t n -> p n t"))
+        positive = keep.tile([P, TILES], F32, name="positive")
+        nc.vector.tensor_scalar(positive[:], cols[:, TILES : 2 * TILES], 0.0, 2.0 * TURN, ALU.is_ge, ALU.mult)
+        signed_turn = keep.tile([P, TILES], F32, name="signed_turn")
+        nc.vector.tensor_scalar(signed_turn[:], positive[:], 1.0, -TURN, ALU.mult, ALU.add)
 
         gather_words(0)
-        w4_w = keep.tile([P, PASSES * TILES * 2 * P], U8, name="w4_w", align_bytes=64)
-        w4_sc = keep.tile([P, PASSES * TILES * P], U8, name="w4_sc", align_bytes=64)
+        w4_w = big.tile([P, PASSES * TILES * 2 * P], U8, name="w4_w", offset=18 * KIB, align_bytes=64)
+        w4_sc = big.tile([P, PASSES * TILES * P], U8, name="w4_sc", offset=22 * KIB, align_bytes=64)
+        nc.vector.memset(w4_sc[:].bitcast(I32), 0)
         nc.vector.tensor_copy(
             w4_w[:].bitcast(I32).rearrange("p (n t g w) -> p n t g w", t=4, g=16, w=4),
             w4_raw[:].rearrange("p a c -> p (a c)").rearrange("p (n g t w) -> p n t g w", t=4, g=16, w=4),
         )
-        nc.vector.tensor_copy(
-            w4_sc[:].bitcast(I32).rearrange("p (n t g w) -> p n t g w", t=4, g=16, w=2),
-            w4_sc_raw[:].rearrange("p a c -> p (a c)").bitcast(I32).rearrange("p (n g t w) -> p n t g w", t=4, g=16, w=2),
-        )
+        for q in range(4):
+            live = slice(32 * q, 32 * q + 4)
+            nc.vector.tensor_copy(
+                w4_sc[live, :].bitcast(I32).rearrange("p (n t g w) -> p n t g w", t=4, g=16, w=2),
+                w4_sc_raw[live].rearrange("p a c -> p (a c)").bitcast(I32).rearrange("p (n g t w) -> p n t g w", t=4, g=16, w=2),
+            )
+
         gather_words(1)
 
         w1_raw = {}
         for b in range(2):
             for a in range(PASSES):
-                raw = big.tile([P, 4, 512], F32, name="w1_raw%d%d" % (a, b), offset=4 * T * b + 2 * T * a)
+                raw = big.tile([P, 4, 512], F32, name="w1_raw%d%d" % (a, b), offset=W1_AT[a, b] * KIB)
                 nc.sync.dma_start(
                     raw[:], w1[512 * a : 512 * (a + 1), 512 * b : 512 * (b + 1)].rearrange("(p j) c -> p j c", j=4)
                 )
                 w1_raw[a, b] = raw
-        client_t = keep.tile([P, 4, NP], F32, name="client_t", tag="w4_raw")
+        client_t = big.tile([P, 4, NP], F32, name="client_t", offset=10 * KIB)
         nc.sync.dma_start(client_t[:], client.rearrange("(u p) j -> p u j", p=P))
 
-        ident = keep.tile([P, P], F32, name="ident")
-        make_identity(nc, ident[:])
-        turned = psum.tile([P, P], F32, name="turned", tag="a")
-        nc.tensor.transpose(turned[:], rows[:], ident[:])
-        cols = keep.tile([P, 2 * TILES + 4], F32, name="cols")
-        nc.vector.tensor_copy(cols[:], turned[:, 0 : 2 * TILES + 4])
-        positive = keep.tile([P, TILES], F32, name="positive")
-        nc.vector.tensor_scalar(positive[:], cols[:, TILES : 2 * TILES], 0.0, 2.0 * TURN, ALU.is_ge, ALU.mult)
-        signed_turn = keep.tile([P, TILES], F32, name="signed_turn")
-        nc.vector.tensor_scalar(signed_turn[:], positive[:], 1.0, -TURN, ALU.mult, ALU.add)
+        d_t = big.tile([P, 4], F32, name="d_t", offset=2 * KIB)
+        with nc.allow_non_contiguous_dma(reason="one offset a partition and row tile"):
+            nc.sync.dma_start(d_t[:], d.rearrange("(u p) -> p u", p=P))
 
         fracs = {}
         picked = {}
@@ -127,10 +140,13 @@ def tile_list_segment_redundancy_scores_kernel(
 
         def reduce_b(n):
             frac = ring.tile([P, S], F32, name="frac")
-            by_vector = n < VECTOR_TILES
+            by_vector = n in VECTOR_TILES
             if not by_vector:
-                turns = ring.tile([P, S], F32, name="turns")
-            whole = ring.tile([P, S], I32, name="whole")
+                turns = ring.tile([P, S], F32, name="turns", tag="scalar_out", bufs=4, align_bytes=64)
+            if n == 0:
+                whole = keep.tile([P, S], I32, name="whole", tag="first", align_bytes=64)
+            else:
+                whole = ring.tile([P, S], I32, name="whole")
             for half in range(2):
                 cs = slice(BANK * half, BANK * (half + 1))
                 acc = psum.tile([P, BANK], F32, name="acc_b", tag="b")
@@ -156,24 +172,30 @@ def tile_list_segment_redundancy_scores_kernel(
             fracs[n] = frac
 
         def sine_of_b(n):
-            sine = ring.tile([P, S], F32, name="sine", bufs=3)
+            sine = ring.tile([P, S], F32, name="sine", tag="scalar_out", bufs=4, align_bytes=64)
             nc.scalar.activation(sine[:], fracs[n][:], ACT.Sin, scale=signed_turn[:, n : n + 1])
             sines[n] = sine
 
-        def quantise_w1(n):
+        rounded = {}
+
+        def cast_w1(n):
             b, t = divmod(n, 4)
-            grouped = ring.tile([P, PASSES, 4 * P], BF16, name="grouped", align_bytes=64)
+            grouped = ring.tile([P, PASSES, 4 * P], BF16, name="grouped", tag="scalar_out", bufs=4, align_bytes=64)
             for a in range(PASSES):
                 nc.scalar.copy(
                     grouped[:, a, :].rearrange("p (g h i j) -> p g h j i", h=2, i=4, j=4),
                     w1_raw[a, b][:].rearrange("p j (g t h i) -> p t g h j i", t=4, h=2, i=4)[:, t],
                 )
-            codes = keep.tile([P, PASSES * P], U32, name="w1_codes%d" % n, align_bytes=64)
+            rounded[n] = grouped
+
+        def quantise_w1(n):
+            grouped = rounded[n]
+            codes = keep.tile([P, PASSES * P], U32, name="w1_codes%d" % n, tag="first" if n == 0 else "w1_codes%d" % n, align_bytes=64)
             scales = keep.tile([P, PASSES * P], U8, name="w1_scales%d" % n, align_bytes=64)
             nc.vector.quantize_mx(out=codes[:].bitcast(FP8X4), scales=scales[:], in_=grouped[:].rearrange("p a c -> p (a c)"))
             w1_q[n] = (codes, scales)
 
-        planes1 = [keep.tile([P, 4, NP], BF16, name="planes1_%d" % b) for b in range(2)]
+        planes1 = [keep.tile([P, 4, NP], F32, name="planes1_%d" % b) for b in range(2)]
         planes2 = [keep.tile([P, 4, NP], BF16, name="planes2_%d" % b) for b in range(2)]
 
         def rows_of_h(n):
@@ -248,29 +270,33 @@ def tile_list_segment_redundancy_scores_kernel(
             weighted = ring.tile([P, NP], F32, name="weighted", bufs=4)
             nc.vector.tensor_tensor(weighted[:], scores[u][:], client_t[:, u, :], ALU.mult)
             scored = ring.tile([P, NP], F32, name="scored", bufs=4)
-            nc.scalar.activation(scored[:], weighted[:], ACT.Identity, bias=cols[:, 2 * TILES + u : 2 * TILES + u + 1])
+            nc.scalar.activation(scored[:], weighted[:], ACT.Identity, bias=d_t[:, u : u + 1])
             nc.sync.dma_start(out[P * u : P * (u + 1), :], scored[:])
 
         for n in range(-2, TILES + 1):
             if n + 2 < TILES:
-                quantise_w1(n + 2)
+                cast_w1(n + 2)
                 reduce_b(n + 2)
+                quantise_w1(n + 2)
             if 0 <= n + 1 < TILES:
                 sine_of_b(n + 1)
             if 0 <= n < TILES:
                 rows_of_h(n)
             if 0 <= n - 1:
                 magnitude(n - 1)
-            if n in (5, 6):
-                which = 2 if n == 5 else 1
-                weave(nc.scalar.copy, which, 0, 0, 256)
-                weave(nc.scalar.copy, which, 0, 256, 512)
-                quantise_x(which, 0, 0, NP)
+            if n == 6:
+                weave(nc.scalar.copy, 2, 0, 0, 256)
+                weave(nc.scalar.copy, 2, 0, 256, 512)
+                quantise_x(2, 0, 0, NP)
+            if n == 7:
+                weave(nc.scalar.copy, 1, 0, 0, 256)
+                weave(nc.scalar.copy, 1, 0, 256, 512)
+                quantise_x(1, 0, 0, NP)
             if n == 7:
                 for u in range(4):
                     score_pass(u, 0)
-        weave(nc.scalar.copy, 2, 1, 0, 192)
-        weave(nc.vector.tensor_copy, 2, 1, 192, NP)
+        weave(nc.scalar.copy, 2, 1, 0, 128)
+        weave(nc.vector.tensor_copy, 2, 1, 128, NP)
         quantise_x(2, 1, 0, NP)
         for half in range(2):
             weave(nc.scalar.copy, 1, 1, 256 * half, 256 * (half + 1))

@@ -86,6 +86,8 @@ def tile_list_segment_redundancy_scores_kernel(
         nc.vector.tensor_copy(v_sc[:], tab_sc[:].indirect(offs_t[:]))
         nc.scalar.dma_start(v_sc1[0:112, :].bitcast(I32), v_sc[4:116, :].bitcast(I32))
         v_planes = (v_sc, v_sc1)
+        warm = keep.tile([P, 1], F32, name="warm")
+        nc.scalar.activation(warm[:], dealt[:, 0, 0:1], ACT.Sin)
         ident = keep.tile([P, P], F32, name="ident")
         make_identity(nc, ident[:])
         nc.vector.tensor_copy(
@@ -295,11 +297,10 @@ def tile_list_segment_redundancy_scores_kernel(
             if n == 7:
                 for u in range(4):
                     score_pass(u, 0)
-        weave(nc.scalar.copy, 2, 1, 0, 128)
-        weave(nc.vector.tensor_copy, 2, 1, 128, NP)
+        weave(nc.vector.tensor_copy, 2, 1, 0, NP)
         quantise_x(2, 1, 0, NP)
-        for half in range(2):
-            weave(nc.scalar.copy, 1, 1, 256 * half, 256 * (half + 1))
-            quantise_x(1, 1, 256 * half, 256 * (half + 1))
-            finish(2 * half)
-            finish(2 * half + 1)
+        for lo, hi in ((0, 256), (256, 512)):
+            weave(nc.scalar.copy, 1, 1, lo, hi)
+            quantise_x(1, 1, lo, hi)
+            for u in range(lo // P, hi // P):
+                finish(u)

@@ -20,13 +20,24 @@ ACT = mybir.ActivationFunctionType
 
 P = 128
 BANK = 512
-PASSES = 2
-TILES = 8
-KIB = 1024
-W1_AT = {(0, 0): 10, (1, 0): 2, (0, 1): 24, (1, 1): 32}
+PASSES = K // BANK
+GROUPS = H // BANK
+TILES = H // P
+HALVES = S // BANK
 TURN = 2.0 * math.pi
 WHOLE = 1.5 * 2.0**23
-VECTOR_TILES = (0, 1, 2)
+
+TILES_COUNTED_BY_VECTOR = 3
+SCALAR_RING = 4
+
+KIB = 1024
+TABLE_AT = (8, 25)
+TABLE_SCALES_AT = 41
+PICKED_AT = (41, 17)
+W4_AT = 21
+W1_AT = {(0, 0): 9, (1, 0): 1, (0, 1): 25, (1, 1): 33}
+CLIENT_AT, D_AT = 9, 1
+COUNTS_AT = 45
 
 
 def tile_list_segment_redundancy_scores_kernel(
@@ -37,269 +48,304 @@ def tile_list_segment_redundancy_scores_kernel(
         lists = ctx.enter_context(tc.tile_pool(name="lists", bufs=1))
         keep = ctx.enter_context(tc.tile_pool(name="keep", bufs=1))
         ring = ctx.enter_context(tc.tile_pool(name="ring", bufs=3))
-        big = ctx.enter_context(tc.tile_pool(name="big", bufs=1))
+        shared = ctx.enter_context(tc.tile_pool(name="shared", bufs=1))
         psum = ctx.enter_context(tc.psum_pool(name="psum", bufs=4))
 
-        tab_sc = keep.tile([P, T], U8, name="tab_sc", tag="picked01", align_bytes=64)
-        rows = keep.tile([P, 512], F32, name="rows", tag="picked00", align_bytes=64)
-        tab_sc_rows = keep.tile([P, T // 4], I32, name="tab_sc_rows")
-        w4_sc_raw = keep.tile([P, PASSES, H], U8, name="w4_sc_raw", tag="picked11", align_bytes=64)
-        dealt = keep.tile([P, 4, P], F32, name="dealt")
-        nc.vector.memset(tab_sc[:].bitcast(I32), 0)
-        nc.gpsimd.memset(dealt[:], 0.0)
-        v_sc1 = keep.tile([P, S], U8, name="v_sc1", align_bytes=64)
-        nc.gpsimd.memset(v_sc1[:].bitcast(I32), 0)
+        table_scales = shared.tile([P, T], U8, name="table_scales", offset=TABLE_SCALES_AT * KIB)
+        vector_rows = keep.tile([P, BANK], F32, name="vector_rows")
+        table_scale_rows = keep.tile([P, T // 4], I32, name="table_scale_rows")
+        w4_scale_rows = keep.tile([P, PASSES, H], U8, name="w4_scale_rows")
+        dealt_rows = keep.tile([P, 4, P], F32, name="dealt_rows")
+        nc.vector.memset(table_scales[:].bitcast(I32), 0)
+        nc.gpsimd.memset(dealt_rows[:], 0.0)
+        v_plane1 = keep.tile([P, S], U8, name="v_plane1", align_bytes=64)
+        nc.gpsimd.memset(v_plane1[:].bitcast(I32), 0)
+        w4_planes = keep.tile([P, PASSES * TILES * P], U8, name="w4_planes", align_bytes=64)
+        nc.gpsimd.memset(w4_planes[:].bitcast(I32), 0)
 
         offs_t = lists.tile([P, S // 16], U16, name="offs_t")
         pos1_t = lists.tile([P, NP // 16], U16, name="pos1_t")
         pos2_t = lists.tile([P, NP // 16], U16, name="pos2_t")
-        tab_w = [big.tile([P, T], I32, name="tab_w%d" % a, offset=(8 + 16 * a) * KIB) for a in range(PASSES)]
-        w4_raw = keep.tile([P, PASSES, H // 2], I32, name="w4_raw", tag="picked10", align_bytes=64)
+        table = [shared.tile([P, T], I32, name="table%d" % a, offset=TABLE_AT[a] * KIB) for a in range(PASSES)]
+        w4_loaded = keep.tile([P, PASSES, H // 2], I32, name="w4_loaded")
         nc.sync.dma_start(offs_t[:], offs)
-        for q in range(4):
-            nc.sync.dma_start(tab_sc_rows[32 * q : 32 * q + 8, :], tab_scales[:, 4 * q : 4 * q + 4, :].bitcast(I32))
-        nc.sync.dma_start(rows[0:2, :], b1.rearrange("(b c) -> b c", b=2))
-        nc.sync.dma_start(rows[2:4, :], gain.rearrange("(b c) -> b c", b=2))
-        nc.sync.dma_start(tab_w[0][:], tab_words[0].rearrange("p t i -> p (t i)").bitcast(I32))
-        nc.sync.dma_start(w4_raw[:], w4_words.rearrange("a p c -> p a c").bitcast(I32))
-        for q in range(4):
+        for quad in range(4):
             nc.sync.dma_start(
-                w4_sc_raw[32 * q : 32 * q + 4, :, :].bitcast(I32),
-                w4_scales[:, 4 * q : 4 * q + 4, :].rearrange("a q c -> q a c").bitcast(I32),
+                table_scale_rows[32 * quad : 32 * quad + 8, :], tab_scales[:, 4 * quad : 4 * quad + 4, :].bitcast(I32)
             )
-        nc.sync.dma_start(tab_w[1][:], tab_words[1].rearrange("p t i -> p (t i)").bitcast(I32))
+        nc.sync.dma_start(vector_rows[0:2, :], b1.rearrange("(b c) -> b c", b=GROUPS))
+        nc.sync.dma_start(vector_rows[2:4, :], gain.rearrange("(b c) -> b c", b=GROUPS))
+        nc.sync.dma_start(table[0][:], tab_words[0].rearrange("p t i -> p (t i)").bitcast(I32))
+        nc.sync.dma_start(w4_loaded[:], w4_words.rearrange("a p c -> p a c").bitcast(I32))
+        for quad in range(4):
+            nc.sync.dma_start(
+                w4_scale_rows[32 * quad : 32 * quad + 4, :, :].bitcast(I32),
+                w4_scales[:, 4 * quad : 4 * quad + 4, :].rearrange("a q c -> q a c").bitcast(I32),
+            )
+        nc.sync.dma_start(table[1][:], tab_words[1].rearrange("p t i -> p (t i)").bitcast(I32))
         nc.sync.dma_start(pos2_t[:], pos2)
         nc.sync.dma_start(pos1_t[:], pos1)
 
-        for q in range(4):
-            nc.vector.tensor_copy(tab_sc[32 * q : 32 * q + 8, :].bitcast(I32), tab_sc_rows[32 * q : 32 * q + 8, :])
+        for quad in range(4):
+            live = slice(32 * quad, 32 * quad + 8)
+            nc.vector.tensor_copy(table_scales[live, :].bitcast(I32), table_scale_rows[live, :])
+        v_plane0 = keep.tile([P, S], U8, name="v_plane0", align_bytes=64)
+        nc.vector.tensor_copy(v_plane0[:], table_scales[:].indirect(offs_t[:]))
+        nc.scalar.dma_start(v_plane1[0:112, :].bitcast(I32), v_plane0[4:116, :].bitcast(I32))
+        v_planes = (v_plane0, v_plane1)
 
-        v_w = {}
-
-        def gather_words(a):
-            for half in range(2):
-                words = keep.tile([P, BANK], U32, name="v_w%d%d" % (a, half), tag="picked%d%d" % (a, half), align_bytes=64)
-                nc.vector.tensor_copy(words[:], tab_w[a][:].bitcast(U32).indirect(offs_t[:, 32 * half : 32 * (half + 1)]))
-                v_w[a, half] = words
-
-        v_sc = keep.tile([P, S], U8, name="v_sc", align_bytes=64)
-        nc.vector.tensor_copy(v_sc[:], tab_sc[:].indirect(offs_t[:]))
-        nc.scalar.dma_start(v_sc1[0:112, :].bitcast(I32), v_sc[4:116, :].bitcast(I32))
-        v_planes = (v_sc, v_sc1)
-        warm = keep.tile([P, 1], F32, name="warm")
-        nc.scalar.activation(warm[:], dealt[:, 0, 0:1], ACT.Sin)
         ident = keep.tile([P, P], F32, name="ident")
         make_identity(nc, ident[:])
-        nc.vector.tensor_copy(
-            dealt[0:4].rearrange("p t (g q) -> p t g q", q=8), rows[0:4, :].rearrange("p (g t q) -> p t g q", t=4, q=8)
+        nc.gpsimd.tensor_copy(
+            dealt_rows[0:4].rearrange("p t (g q) -> p t g q", q=8),
+            vector_rows[0:4, :].rearrange("p (g t q) -> p t g q", t=4, q=8),
         )
         turned = psum.tile([P, 4, P], F32, name="turned", tag="a")
         for t in range(4):
-            nc.tensor.transpose(turned[:, t, :], dealt[:, t, :], ident[:])
-        cols = keep.tile([P, 2 * TILES], F32, name="cols")
-        nc.vector.tensor_copy(cols[:].rearrange("p (n t) -> p n t", t=4), turned[:, :, 0:4].rearrange("p t n -> p n t"))
+            nc.tensor.transpose(turned[:, t, :], dealt_rows[:, t, :], ident[:])
+        per_row = keep.tile([P, 2 * TILES], F32, name="per_row")
+        nc.vector.tensor_copy(
+            per_row[:].rearrange("p (n t) -> p n t", t=4), turned[:, :, 0:4].rearrange("p t n -> p n t")
+        )
         positive = keep.tile([P, TILES], F32, name="positive")
-        nc.vector.tensor_scalar(positive[:], cols[:, TILES : 2 * TILES], 0.0, 2.0 * TURN, ALU.is_ge, ALU.mult)
+        nc.gpsimd.tensor_scalar(positive[:], per_row[:, TILES : 2 * TILES], 0.0, 2.0 * TURN, ALU.is_ge, ALU.mult)
         signed_turn = keep.tile([P, TILES], F32, name="signed_turn")
-        nc.vector.tensor_scalar(signed_turn[:], positive[:], 1.0, -TURN, ALU.mult, ALU.add)
+        nc.gpsimd.tensor_scalar(signed_turn[:], positive[:], 1.0, -TURN, ALU.mult, ALU.add)
+
+        v_words = {}
+
+        def gather_words(a):
+            for half in range(HALVES):
+                words = shared.tile(
+                    [P, BANK], U32, name="v_words%d%d" % (a, half), offset=(PICKED_AT[a] + 2 * half) * KIB, align_bytes=64
+                )
+                entries = offs_t[:, (BANK // 16) * half : (BANK // 16) * (half + 1)]
+                nc.vector.tensor_copy(words[:], table[a][:].bitcast(U32).indirect(entries))
+                v_words[a, half] = words
 
         gather_words(0)
-        w4_w = big.tile([P, PASSES * TILES * 2 * P], U8, name="w4_w", offset=18 * KIB, align_bytes=64)
-        w4_sc = big.tile([P, PASSES * TILES * P], U8, name="w4_sc", offset=22 * KIB, align_bytes=64)
-        nc.vector.memset(w4_sc[:].bitcast(I32), 0)
+
+        w4_dealt = shared.tile([P, PASSES * TILES * 2 * P], U8, name="w4_dealt", offset=W4_AT * KIB, align_bytes=64)
         nc.vector.tensor_copy(
-            w4_w[:].bitcast(I32).rearrange("p (n t g w) -> p n t g w", t=4, g=16, w=4),
-            w4_raw[:].rearrange("p a c -> p (a c)").rearrange("p (n g t w) -> p n t g w", t=4, g=16, w=4),
+            w4_dealt[:].bitcast(I32).rearrange("p (n t g w) -> p n t g w", t=4, g=16, w=4),
+            w4_loaded[:].rearrange("p a c -> p (a c)").rearrange("p (n g t w) -> p n t g w", t=4, g=16, w=4),
         )
-        for q in range(4):
-            live = slice(32 * q, 32 * q + 4)
-            nc.vector.tensor_copy(
-                w4_sc[live, :].bitcast(I32).rearrange("p (n t g w) -> p n t g w", t=4, g=16, w=2),
-                w4_sc_raw[live].rearrange("p a c -> p (a c)").bitcast(I32).rearrange("p (n g t w) -> p n t g w", t=4, g=16, w=2),
+        for quad in range(4):
+            live = slice(32 * quad, 32 * quad + 4)
+            nc.gpsimd.tensor_copy(
+                w4_planes[live, :].bitcast(I32).rearrange("p (n t g w) -> p n t g w", t=4, g=16, w=2),
+                w4_scale_rows[live]
+                .rearrange("p a c -> p (a c)")
+                .bitcast(I32)
+                .rearrange("p (n g t w) -> p n t g w", t=4, g=16, w=2),
             )
 
         gather_words(1)
 
-        w1_raw = {}
-        for b in range(2):
+        w1_loaded = {}
+        for b in range(GROUPS):
             for a in range(PASSES):
-                raw = big.tile([P, 4, 512], F32, name="w1_raw%d%d" % (a, b), offset=W1_AT[a, b] * KIB)
+                part = shared.tile([P, 4, BANK], F32, name="w1_loaded%d%d" % (a, b), offset=W1_AT[a, b] * KIB)
                 nc.sync.dma_start(
-                    raw[:], w1[512 * a : 512 * (a + 1), 512 * b : 512 * (b + 1)].rearrange("(p j) c -> p j c", j=4)
+                    part[:], w1[BANK * a : BANK * (a + 1), BANK * b : BANK * (b + 1)].rearrange("(p i) c -> p i c", i=4)
                 )
-                w1_raw[a, b] = raw
-        client_t = big.tile([P, 4, NP], F32, name="client_t", offset=10 * KIB)
+                w1_loaded[a, b] = part
+        client_t = shared.tile([P, NP // P, NP], F32, name="client_t", offset=CLIENT_AT * KIB)
         nc.sync.dma_start(client_t[:], client.rearrange("(u p) j -> p u j", p=P))
-
-        d_t = big.tile([P, 4], F32, name="d_t", offset=2 * KIB)
-        with nc.allow_non_contiguous_dma(reason="one offset a partition and row tile"):
+        d_t = shared.tile([P, NP // P], F32, name="d_t", offset=D_AT * KIB)
+        with nc.allow_non_contiguous_dma(reason="one value of d for each partition and output tile"):
             nc.sync.dma_start(d_t[:], d.rearrange("(u p) -> p u", p=P))
 
-        fracs = {}
-        picked = {}
+        fractions = {}
         sines = {}
-        w1_q = {}
+        w1_rounded = {}
+        w1_quantised = {}
+        picked_for_x2 = {}
 
-        def reduce_b(n):
-            frac = ring.tile([P, S], F32, name="frac")
-            by_vector = n in VECTOR_TILES
+        def fraction_of_turn(n):
+            fraction = ring.tile([P, S], F32, name="fraction")
+            by_vector = n < TILES_COUNTED_BY_VECTOR
             if not by_vector:
-                turns = ring.tile([P, S], F32, name="turns", tag="scalar_out", bufs=4, align_bytes=64)
-            if n == 0:
-                whole = keep.tile([P, S], I32, name="whole", tag="first", align_bytes=64)
+                turns = ring.tile([P, S], F32, name="turns", tag="scalar_out", bufs=SCALAR_RING, align_bytes=64)
+            if n < 2:
+                count = shared.tile([P, S], I32, name="count%d" % n, offset=(COUNTS_AT + 4 * n) * KIB)
             else:
-                whole = ring.tile([P, S], I32, name="whole")
-            for half in range(2):
-                cs = slice(BANK * half, BANK * (half + 1))
-                acc = psum.tile([P, BANK], F32, name="acc_b", tag="b")
+                count = ring.tile([P, S], I32, name="count")
+            for half in range(HALVES):
+                cols = slice(BANK * half, BANK * (half + 1))
+                sum_b = psum.tile([P, BANK], F32, name="sum_b", tag="b")
                 for a in range(PASSES):
                     at = a * TILES + n
                     nc.tensor.matmul_mx(
-                        out=acc[:],
-                        lhsT=w4_w[:, 2 * P * at : 2 * P * (at + 1)].bitcast(FP4X4),
-                        lhsT_scale=w4_sc[:, P * at : P * (at + 1)],
-                        rhs=v_w[a, half][:].bitcast(FP8X4),
-                        rhs_scale=v_planes[a][:, cs],
+                        out=sum_b[:],
+                        lhsT=w4_dealt[:, 2 * P * at : 2 * P * (at + 1)].bitcast(FP4X4),
+                        lhsT_scale=w4_planes[:, P * at : P * (at + 1)],
+                        rhs=v_words[a, half][:].bitcast(FP8X4),
+                        rhs_scale=v_planes[a][:, cols],
                         start=(a == 0),
                         stop=(a == PASSES - 1),
                     )
                 if by_vector:
-                    nc.vector.tensor_scalar(whole[:, cs], acc[:], 1.0 / TURN, None, ALU.mult)
-                    nc.vector.scalar_tensor_tensor(frac[:, cs], acc[:], 1.0 / TURN, whole[:, cs], ALU.mult, ALU.subtract)
+                    nc.vector.tensor_scalar(count[:, cols], sum_b[:], 1.0 / TURN, None, ALU.mult)
+                    nc.vector.scalar_tensor_tensor(
+                        fraction[:, cols], sum_b[:], 1.0 / TURN, count[:, cols], ALU.mult, ALU.subtract
+                    )
                 else:
-                    nc.scalar.activation(turns[:, cs], acc[:], ACT.Copy, scale=-1.0 / TURN)
+                    nc.scalar.activation(turns[:, cols], sum_b[:], ACT.Copy, scale=-1.0 / TURN)
             if not by_vector:
-                nc.scalar.activation(whole[:].bitcast(U32), turns[:], ACT.Copy, bias=WHOLE)
-                nc.vector.scalar_tensor_tensor(frac[:], whole[:], WHOLE, turns[:], ALU.subtract, ALU.subtract)
-            fracs[n] = frac
+                nc.scalar.activation(count[:].bitcast(U32), turns[:], ACT.Copy, bias=WHOLE)
+                nc.vector.scalar_tensor_tensor(fraction[:], count[:], WHOLE, turns[:], ALU.subtract, ALU.subtract)
+            fractions[n] = fraction
 
-        def sine_of_b(n):
-            sine = ring.tile([P, S], F32, name="sine", tag="scalar_out", bufs=4, align_bytes=64)
-            nc.scalar.activation(sine[:], fracs[n][:], ACT.Sin, scale=signed_turn[:, n : n + 1])
-            sines[n] = sine
+        def sine(n):
+            values = ring.tile([P, S], F32, name="sine", tag="scalar_out", bufs=SCALAR_RING, align_bytes=64)
+            nc.scalar.activation(values[:], fractions[n][:], ACT.Sin, scale=signed_turn[:, n : n + 1])
+            sines[n] = values
 
-        rounded = {}
-
-        def cast_w1(n):
+        def round_w1(n):
             b, t = divmod(n, 4)
-            grouped = ring.tile([P, PASSES, 4 * P], BF16, name="grouped", tag="scalar_out", bufs=4, align_bytes=64)
+            if b == 0:
+                rounded = shared.tile(
+                    [P, PASSES, 4 * P], BF16, name="rounded%d" % n, offset=(COUNTS_AT + 2 * n) * KIB, align_bytes=64
+                )
+            else:
+                rounded = ring.tile(
+                    [P, PASSES, 4 * P], BF16, name="rounded", tag="scalar_out", bufs=SCALAR_RING, align_bytes=64
+                )
             for a in range(PASSES):
                 nc.scalar.copy(
-                    grouped[:, a, :].rearrange("p (g h i j) -> p g h j i", h=2, i=4, j=4),
-                    w1_raw[a, b][:].rearrange("p j (g t h i) -> p t g h j i", t=4, h=2, i=4)[:, t],
+                    rounded[:, a, :].rearrange("p (g e c i) -> p g e i c", e=2, c=4, i=4),
+                    w1_loaded[a, b][:].rearrange("p i (g t e c) -> p t g e i c", t=4, e=2, c=4)[:, t],
                 )
-            rounded[n] = grouped
+            w1_rounded[n] = rounded
 
         def quantise_w1(n):
-            grouped = rounded[n]
-            codes = keep.tile([P, PASSES * P], U32, name="w1_codes%d" % n, tag="first" if n == 0 else "w1_codes%d" % n, align_bytes=64)
+            codes = keep.tile([P, PASSES * P], U32, name="w1_codes%d" % n, align_bytes=64)
             scales = keep.tile([P, PASSES * P], U8, name="w1_scales%d" % n, align_bytes=64)
-            nc.vector.quantize_mx(out=codes[:].bitcast(FP8X4), scales=scales[:], in_=grouped[:].rearrange("p a c -> p (a c)"))
-            w1_q[n] = (codes, scales)
+            nc.vector.quantize_mx(
+                out=codes[:].bitcast(FP8X4), scales=scales[:], in_=w1_rounded[n][:].rearrange("p a c -> p (a c)")
+            )
+            w1_quantised[n] = (codes, scales)
 
-        planes1 = [keep.tile([P, 4, NP], F32, name="planes1_%d" % b) for b in range(2)]
-        planes2 = [keep.tile([P, 4, NP], BF16, name="planes2_%d" % b) for b in range(2)]
+        x_tiles = {
+            1: [keep.tile([P, 4, NP], F32, name="x1_tiles%d" % b) for b in range(GROUPS)],
+            2: [keep.tile([P, 4, NP], BF16, name="x2_tiles%d" % b) for b in range(GROUPS)],
+        }
 
         def rows_of_h(n):
             b, t = divmod(n, 4)
-            codes, scales = w1_q[n]
+            codes, scales = w1_quantised[n]
             h = ring.tile([P, S], F32, name="h")
-            for half in range(2):
-                cs = slice(BANK * half, BANK * (half + 1))
-                acc = psum.tile([P, BANK], F32, name="acc_a", tag="a")
+            for half in range(HALVES):
+                cols = slice(BANK * half, BANK * (half + 1))
+                sum_a = psum.tile([P, BANK], F32, name="sum_a", tag="a")
                 for a in range(PASSES):
                     nc.tensor.matmul_mx(
-                        out=acc[:],
+                        out=sum_a[:],
                         lhsT=codes[:, P * a : P * (a + 1)].bitcast(FP8X4),
                         lhsT_scale=scales[:, P * a : P * (a + 1)],
-                        rhs=v_w[a, half][:].bitcast(FP8X4),
-                        rhs_scale=v_planes[a][:, cs],
+                        rhs=v_words[a, half][:].bitcast(FP8X4),
+                        rhs_scale=v_planes[a][:, cols],
                         start=(a == 0),
                         stop=(a == PASSES - 1),
                     )
-                nc.vector.scalar_tensor_tensor(h[:, cs], acc[:], cols[:, n : n + 1], sines[n][:, cs], ALU.add, ALU.mult)
-            picked2 = ring.tile([P, NP], F32, name="picked2")
-            nc.vector.tensor_copy(picked2[:], h[:].indirect(pos2_t[:]))
-            nc.vector.tensor_copy(planes1[b][:, t, :], h[:].indirect(pos1_t[:]))
-            picked[n] = picked2
+                nc.vector.scalar_tensor_tensor(
+                    h[:, cols], sum_a[:], per_row[:, n : n + 1], sines[n][:, cols], ALU.add, ALU.mult
+                )
+            picked = ring.tile([P, NP], F32, name="picked")
+            nc.vector.tensor_copy(picked[:], h[:].indirect(pos2_t[:]))
+            nc.vector.tensor_copy(x_tiles[1][b][:, t, :], h[:].indirect(pos1_t[:]))
+            picked_for_x2[n] = picked
 
         def magnitude(n):
             b, t = divmod(n, 4)
-            nc.scalar.activation(planes2[b][:, t, :], picked[n][:], ACT.Abs, scale=cols[:, TILES + n : TILES + n + 1])
+            nc.scalar.activation(
+                x_tiles[2][b][:, t, :], picked_for_x2[n][:], ACT.Abs, scale=per_row[:, TILES + n : TILES + n + 1]
+            )
 
         woven = {}
-        x_q = {}
+        x_quantised = {}
         for which in (1, 2):
-            for b in range(2):
+            for b in range(GROUPS):
                 woven[which, b] = keep.tile([P, NP, 4], BF16, name="woven%d_%d" % (which, b), align_bytes=64)
-                x_q[which, b] = (
+                x_quantised[which, b] = (
                     keep.tile([P, NP], U32, name="x_codes%d_%d" % (which, b), align_bytes=64),
                     keep.tile([P, NP], U8, name="x_scales%d_%d" % (which, b), align_bytes=64),
                 )
-        planes = {1: planes1, 2: planes2}
 
         def weave(copy, which, b, lo, hi):
             copy(
-                woven[which, b][:, lo:hi, :].rearrange("p (c i) t -> p c t i", i=4),
-                planes[which][b][:, :, lo:hi].rearrange("p t (c i) -> p c t i", i=4),
+                woven[which, b][:, lo:hi, :].rearrange("p (e c) t -> p e t c", c=4),
+                x_tiles[which][b][:, :, lo:hi].rearrange("p t (e c) -> p e t c", c=4),
             )
 
         def quantise_x(which, b, lo, hi):
-            codes, scales = x_q[which, b]
+            codes, scales = x_quantised[which, b]
             nc.vector.quantize_mx(
                 out=codes[:, lo:hi].bitcast(FP8X4),
                 scales=scales[:, lo:hi],
                 in_=woven[which, b][:, lo:hi, :].rearrange("p c t -> p (c t)"),
             )
 
-        scores = []
+        def weave_and_quantise_group0(which):
+            weave(nc.scalar.copy, which, 0, 0, NP // 2)
+            weave(nc.scalar.copy, which, 0, NP // 2, NP)
+            quantise_x(which, 0, 0, NP)
+
+        sums_e = []
 
         def score_pass(u, b):
             if b == 0:
-                scores.append(psum.tile([P, NP], F32, name="acc_e", tag="b"))
+                sums_e.append(psum.tile([P, NP], F32, name="sum_e", tag="b"))
             nc.tensor.matmul_mx(
-                out=scores[u][:],
-                lhsT=x_q[1, b][0][:, P * u : P * (u + 1)].bitcast(FP8X4),
-                lhsT_scale=x_q[1, b][1][:, P * u : P * (u + 1)],
-                rhs=x_q[2, b][0][:].bitcast(FP8X4),
-                rhs_scale=x_q[2, b][1][:],
+                out=sums_e[u][:],
+                lhsT=x_quantised[1, b][0][:, P * u : P * (u + 1)].bitcast(FP8X4),
+                lhsT_scale=x_quantised[1, b][1][:, P * u : P * (u + 1)],
+                rhs=x_quantised[2, b][0][:].bitcast(FP8X4),
+                rhs_scale=x_quantised[2, b][1][:],
                 start=(b == 0),
-                stop=(b == 1),
+                stop=(b == GROUPS - 1),
             )
 
         def finish(u):
             score_pass(u, 1)
-            weighted = ring.tile([P, NP], F32, name="weighted", bufs=4)
-            nc.vector.tensor_tensor(weighted[:], scores[u][:], client_t[:, u, :], ALU.mult)
-            scored = ring.tile([P, NP], F32, name="scored", bufs=4)
+            weighted = ring.tile([P, NP], F32, name="weighted", bufs=NP // P)
+            nc.vector.tensor_tensor(weighted[:], sums_e[u][:], client_t[:, u, :], ALU.mult)
+            scored = ring.tile([P, NP], F32, name="scored", bufs=NP // P)
             nc.scalar.activation(scored[:], weighted[:], ACT.Identity, bias=d_t[:, u : u + 1])
             nc.sync.dma_start(out[P * u : P * (u + 1), :], scored[:])
 
-        for n in range(-2, TILES + 1):
-            if n + 2 < TILES:
-                cast_w1(n + 2)
-                reduce_b(n + 2)
-                quantise_w1(n + 2)
-            if 0 <= n + 1 < TILES:
-                sine_of_b(n + 1)
+        fraction_of_turn(0)
+        sine(0)
+        round_w1(0)
+        quantise_w1(0)
+        for n in range(-1, TILES + 1):
+            ahead = n + 2
+            if ahead < TILES_COUNTED_BY_VECTOR:
+                fraction_of_turn(ahead)
+                round_w1(ahead)
+                quantise_w1(ahead)
+            elif ahead < TILES:
+                round_w1(ahead)
+                fraction_of_turn(ahead)
+                quantise_w1(ahead)
+            if 1 <= n + 1 < TILES:
+                sine(n + 1)
             if 0 <= n < TILES:
                 rows_of_h(n)
             if 0 <= n - 1:
                 magnitude(n - 1)
-            if n == 6:
-                weave(nc.scalar.copy, 2, 0, 0, 256)
-                weave(nc.scalar.copy, 2, 0, 256, 512)
-                quantise_x(2, 0, 0, NP)
-            if n == 7:
-                weave(nc.scalar.copy, 1, 0, 0, 256)
-                weave(nc.scalar.copy, 1, 0, 256, 512)
-                quantise_x(1, 0, 0, NP)
-            if n == 7:
-                for u in range(4):
+            if n == TILES - 2:
+                weave_and_quantise_group0(2)
+            if n == TILES - 1:
+                weave_and_quantise_group0(1)
+                for u in range(NP // P):
                     score_pass(u, 0)
+
         weave(nc.vector.tensor_copy, 2, 1, 0, NP)
         quantise_x(2, 1, 0, NP)
-        for lo, hi in ((0, 256), (256, 512)):
+        for lo in range(0, NP, NP // 2):
+            hi = lo + NP // 2
             weave(nc.scalar.copy, 1, 1, lo, hi)
             quantise_x(1, 1, lo, hi)
             for u in range(lo // P, hi // P):

from contextlib import ExitStack
import math

import concourse.mybir as mybir
from concourse.masks import make_identity

K, T, S, H, NP = 1024, 4096, 1024, 1024, 512
FLOPS = 2 * (2 * K * H * S + H * NP * NP)

F32 = mybir.dt.float32
BF16 = mybir.dt.bfloat16
I32 = mybir.dt.int32
U32 = mybir.dt.uint32
U16 = mybir.dt.uint16
U8 = mybir.dt.uint8
FP8X4 = mybir.dt.float8_e4m3fn_x4
FP4X4 = mybir.dt.float4_e2m1fn_x4
ALU = mybir.AluOpType
ACT = mybir.ActivationFunctionType

P = 128
BANK = 512
PASSES = K // BANK
GROUPS = H // BANK
TILES = H // P
HALVES = S // BANK
TURN = 2.0 * math.pi
WHOLE = 1.5 * 2.0**23

TILES_COUNTED_BY_VECTOR = 3
SCALAR_RING = 4

KIB = 1024
TABLE_AT = (8, 25)
TABLE_SCALES_AT = 41
PICKED_AT = (41, 17)
W4_AT = 21
W1_AT = {(0, 0): 9, (1, 0): 1, (0, 1): 25, (1, 1): 33}
CLIENT_AT, D_AT = 9, 1
COUNTS_AT = 45


def tile_list_segment_redundancy_scores_kernel(
    tc, tab_words, tab_scales, offs, pos1, pos2, w1, b1, w4_words, w4_scales, gain, client, d, out
):
    nc = tc.nc
    with ExitStack() as ctx:
        lists = ctx.enter_context(tc.tile_pool(name="lists", bufs=1))
        keep = ctx.enter_context(tc.tile_pool(name="keep", bufs=1))
        ring = ctx.enter_context(tc.tile_pool(name="ring", bufs=3))
        shared = ctx.enter_context(tc.tile_pool(name="shared", bufs=1))
        psum = ctx.enter_context(tc.psum_pool(name="psum", bufs=4))

        table_scales = shared.tile([P, T], U8, name="table_scales", offset=TABLE_SCALES_AT * KIB)
        vector_rows = keep.tile([P, BANK], F32, name="vector_rows")
        table_scale_rows = keep.tile([P, T // 4], I32, name="table_scale_rows")
        w4_scale_rows = keep.tile([P, PASSES, H], U8, name="w4_scale_rows")
        dealt_rows = keep.tile([P, 4, P], F32, name="dealt_rows")
        nc.vector.memset(table_scales[:].bitcast(I32), 0)
        nc.gpsimd.memset(dealt_rows[:], 0.0)
        v_plane1 = keep.tile([P, S], U8, name="v_plane1", align_bytes=64)
        nc.gpsimd.memset(v_plane1[:].bitcast(I32), 0)
        w4_planes = keep.tile([P, PASSES * TILES * P], U8, name="w4_planes", align_bytes=64)
        nc.gpsimd.memset(w4_planes[:].bitcast(I32), 0)

        offs_t = lists.tile([P, S // 16], U16, name="offs_t")
        pos1_t = lists.tile([P, NP // 16], U16, name="pos1_t")
        pos2_t = lists.tile([P, NP // 16], U16, name="pos2_t")
        table = [shared.tile([P, T], I32, name="table%d" % a, offset=TABLE_AT[a] * KIB) for a in range(PASSES)]
        w4_loaded = keep.tile([P, PASSES, H // 2], I32, name="w4_loaded")
        nc.sync.dma_start(offs_t[:], offs)
        for quad in range(4):
            nc.sync.dma_start(
                table_scale_rows[32 * quad : 32 * quad + 8, :], tab_scales[:, 4 * quad : 4 * quad + 4, :].bitcast(I32)
            )
        nc.sync.dma_start(vector_rows[0:2, :], b1.rearrange("(b c) -> b c", b=GROUPS))
        nc.sync.dma_start(vector_rows[2:4, :], gain.rearrange("(b c) -> b c", b=GROUPS))
        nc.sync.dma_start(table[0][:], tab_words[0].rearrange("p t i -> p (t i)").bitcast(I32))
        nc.sync.dma_start(w4_loaded[:], w4_words.rearrange("a p c -> p a c").bitcast(I32))
        for quad in range(4):
            nc.sync.dma_start(
                w4_scale_rows[32 * quad : 32 * quad + 4, :, :].bitcast(I32),
                w4_scales[:, 4 * quad : 4 * quad + 4, :].rearrange("a q c -> q a c").bitcast(I32),
            )
        nc.sync.dma_start(table[1][:], tab_words[1].rearrange("p t i -> p (t i)").bitcast(I32))
        nc.sync.dma_start(pos2_t[:], pos2)
        nc.sync.dma_start(pos1_t[:], pos1)

        for quad in range(4):
            live = slice(32 * quad, 32 * quad + 8)
            nc.vector.tensor_copy(table_scales[live, :].bitcast(I32), table_scale_rows[live, :])
        v_plane0 = keep.tile([P, S], U8, name="v_plane0", align_bytes=64)
        nc.vector.tensor_copy(v_plane0[:], table_scales[:].indirect(offs_t[:]))
        nc.scalar.dma_start(v_plane1[0:112, :].bitcast(I32), v_plane0[4:116, :].bitcast(I32))
        v_planes = (v_plane0, v_plane1)

        ident = keep.tile([P, P], F32, name="ident")
        make_identity(nc, ident[:])
        nc.gpsimd.tensor_copy(
            dealt_rows[0:4].rearrange("p t (g q) -> p t g q", q=8),
            vector_rows[0:4, :].rearrange("p (g t q) -> p t g q", t=4, q=8),
        )
        turned = psum.tile([P, 4, P], F32, name="turned", tag="a")
        for t in range(4):
            nc.tensor.transpose(turned[:, t, :], dealt_rows[:, t, :], ident[:])
        per_row = keep.tile([P, 2 * TILES], F32, name="per_row")
        nc.vector.tensor_copy(
            per_row[:].rearrange("p (n t) -> p n t", t=4), turned[:, :, 0:4].rearrange("p t n -> p n t")
        )
        positive = keep.tile([P, TILES], F32, name="positive")
        nc.gpsimd.tensor_scalar(positive[:], per_row[:, TILES : 2 * TILES], 0.0, 2.0 * TURN, ALU.is_ge, ALU.mult)
        signed_turn = keep.tile([P, TILES], F32, name="signed_turn")
        nc.gpsimd.tensor_scalar(signed_turn[:], positive[:], 1.0, -TURN, ALU.mult, ALU.add)

        v_words = {}

        def gather_words(a):
            for half in range(HALVES):
                words = shared.tile(
                    [P, BANK], U32, name="v_words%d%d" % (a, half), offset=(PICKED_AT[a] + 2 * half) * KIB, align_bytes=64
                )
                entries = offs_t[:, (BANK // 16) * half : (BANK // 16) * (half + 1)]
                nc.vector.tensor_copy(words[:], table[a][:].bitcast(U32).indirect(entries))
                v_words[a, half] = words

        gather_words(0)

        w4_dealt = shared.tile([P, PASSES * TILES * 2 * P], U8, name="w4_dealt", offset=W4_AT * KIB, align_bytes=64)
        nc.vector.tensor_copy(
            w4_dealt[:].bitcast(I32).rearrange("p (n t g w) -> p n t g w", t=4, g=16, w=4),
            w4_loaded[:].rearrange("p a c -> p (a c)").rearrange("p (n g t w) -> p n t g w", t=4, g=16, w=4),
        )
        for quad in range(4):
            live = slice(32 * quad, 32 * quad + 4)
            nc.gpsimd.tensor_copy(
                w4_planes[live, :].bitcast(I32).rearrange("p (n t g w) -> p n t g w", t=4, g=16, w=2),
                w4_scale_rows[live]
                .rearrange("p a c -> p (a c)")
                .bitcast(I32)
                .rearrange("p (n g t w) -> p n t g w", t=4, g=16, w=2),
            )

        gather_words(1)

        w1_loaded = {}
        for b in range(GROUPS):
            for a in range(PASSES):
                part = shared.tile([P, 4, BANK], F32, name="w1_loaded%d%d" % (a, b), offset=W1_AT[a, b] * KIB)
                nc.sync.dma_start(
                    part[:], w1[BANK * a : BANK * (a + 1), BANK * b : BANK * (b + 1)].rearrange("(p i) c -> p i c", i=4)
                )
                w1_loaded[a, b] = part
        client_t = shared.tile([P, NP // P, NP], F32, name="client_t", offset=CLIENT_AT * KIB)
        nc.sync.dma_start(client_t[:], client.rearrange("(u p) j -> p u j", p=P))
        d_t = shared.tile([P, NP // P], F32, name="d_t", offset=D_AT * KIB)
        with nc.allow_non_contiguous_dma(reason="one value of d for each partition and output tile"):
            nc.sync.dma_start(d_t[:], d.rearrange("(u p) -> p u", p=P))

        fractions = {}
        sines = {}
        w1_rounded = {}
        w1_quantised = {}
        picked_for_x2 = {}

        def fraction_of_turn(n):
            fraction = ring.tile([P, S], F32, name="fraction")
            by_vector = n < TILES_COUNTED_BY_VECTOR
            if not by_vector:
                turns = ring.tile([P, S], F32, name="turns", tag="scalar_out", bufs=SCALAR_RING, align_bytes=64)
            if n < 2:
                count = shared.tile([P, S], I32, name="count%d" % n, offset=(COUNTS_AT + 4 * n) * KIB)
            else:
                count = ring.tile([P, S], I32, name="count")
            for half in range(HALVES):
                cols = slice(BANK * half, BANK * (half + 1))
                sum_b = psum.tile([P, BANK], F32, name="sum_b", tag="b")
                for a in range(PASSES):
                    at = a * TILES + n
                    nc.tensor.matmul_mx(
                        out=sum_b[:],
                        lhsT=w4_dealt[:, 2 * P * at : 2 * P * (at + 1)].bitcast(FP4X4),
                        lhsT_scale=w4_planes[:, P * at : P * (at + 1)],
                        rhs=v_words[a, half][:].bitcast(FP8X4),
                        rhs_scale=v_planes[a][:, cols],
                        start=(a == 0),
                        stop=(a == PASSES - 1),
                    )
                if by_vector:
                    nc.vector.tensor_scalar(count[:, cols], sum_b[:], 1.0 / TURN, None, ALU.mult)
                    nc.vector.scalar_tensor_tensor(
                        fraction[:, cols], sum_b[:], 1.0 / TURN, count[:, cols], ALU.mult, ALU.subtract
                    )
                else:
                    nc.scalar.activation(turns[:, cols], sum_b[:], ACT.Copy, scale=-1.0 / TURN)
            if not by_vector:
                nc.scalar.activation(count[:].bitcast(U32), turns[:], ACT.Copy, bias=WHOLE)
                nc.vector.scalar_tensor_tensor(fraction[:], count[:], WHOLE, turns[:], ALU.subtract, ALU.subtract)
            fractions[n] = fraction

        def sine(n):
            values = ring.tile([P, S], F32, name="sine", tag="scalar_out", bufs=SCALAR_RING, align_bytes=64)
            nc.scalar.activation(values[:], fractions[n][:], ACT.Sin, scale=signed_turn[:, n : n + 1])
            sines[n] = values

        def round_w1(n):
            b, t = divmod(n, 4)
            if b == 0:
                rounded = shared.tile(
                    [P, PASSES, 4 * P], BF16, name="rounded%d" % n, offset=(COUNTS_AT + 2 * n) * KIB, align_bytes=64
                )
            else:
                rounded = ring.tile(
                    [P, PASSES, 4 * P], BF16, name="rounded", tag="scalar_out", bufs=SCALAR_RING, align_bytes=64
                )
            for a in range(PASSES):
                nc.scalar.copy(
                    rounded[:, a, :].rearrange("p (g e c i) -> p g e i c", e=2, c=4, i=4),
                    w1_loaded[a, b][:].rearrange("p i (g t e c) -> p t g e i c", t=4, e=2, c=4)[:, t],
                )
            w1_rounded[n] = rounded

        def quantise_w1(n):
            codes = keep.tile([P, PASSES * P], U32, name="w1_codes%d" % n, align_bytes=64)
            scales = keep.tile([P, PASSES * P], U8, name="w1_scales%d" % n, align_bytes=64)
            nc.vector.quantize_mx(
                out=codes[:].bitcast(FP8X4), scales=scales[:], in_=w1_rounded[n][:].rearrange("p a c -> p (a c)")
            )
            w1_quantised[n] = (codes, scales)

        x_tiles = {
            1: [keep.tile([P, 4, NP], F32, name="x1_tiles%d" % b) for b in range(GROUPS)],
            2: [keep.tile([P, 4, NP], BF16, name="x2_tiles%d" % b) for b in range(GROUPS)],
        }

        def rows_of_h(n):
            b, t = divmod(n, 4)
            codes, scales = w1_quantised[n]
            h = ring.tile([P, S], F32, name="h")
            for half in range(HALVES):
                cols = slice(BANK * half, BANK * (half + 1))
                sum_a = psum.tile([P, BANK], F32, name="sum_a", tag="a")
                for a in range(PASSES):
                    nc.tensor.matmul_mx(
                        out=sum_a[:],
                        lhsT=codes[:, P * a : P * (a + 1)].bitcast(FP8X4),
                        lhsT_scale=scales[:, P * a : P * (a + 1)],
                        rhs=v_words[a, half][:].bitcast(FP8X4),
                        rhs_scale=v_planes[a][:, cols],
                        start=(a == 0),
                        stop=(a == PASSES - 1),
                    )
                nc.vector.scalar_tensor_tensor(
                    h[:, cols], sum_a[:], per_row[:, n : n + 1], sines[n][:, cols], ALU.add, ALU.mult
                )
            picked = ring.tile([P, NP], F32, name="picked")
            nc.vector.tensor_copy(picked[:], h[:].indirect(pos2_t[:]))
            nc.vector.tensor_copy(x_tiles[1][b][:, t, :], h[:].indirect(pos1_t[:]))
            picked_for_x2[n] = picked

        def magnitude(n):
            b, t = divmod(n, 4)
            nc.scalar.activation(
                x_tiles[2][b][:, t, :], picked_for_x2[n][:], ACT.Abs, scale=per_row[:, TILES + n : TILES + n + 1]
            )

        woven = {}
        x_quantised = {}
        for which in (1, 2):
            for b in range(GROUPS):
                woven[which, b] = keep.tile([P, NP, 4], BF16, name="woven%d_%d" % (which, b), align_bytes=64)
                x_quantised[which, b] = (
                    keep.tile([P, NP], U32, name="x_codes%d_%d" % (which, b), align_bytes=64),
                    keep.tile([P, NP], U8, name="x_scales%d_%d" % (which, b), align_bytes=64),
                )

        def weave(copy, which, b, lo, hi):
            copy(
                woven[which, b][:, lo:hi, :].rearrange("p (e c) t -> p e t c", c=4),
                x_tiles[which][b][:, :, lo:hi].rearrange("p t (e c) -> p e t c", c=4),
            )

        def quantise_x(which, b, lo, hi):
            codes, scales = x_quantised[which, b]
            nc.vector.quantize_mx(
                out=codes[:, lo:hi].bitcast(FP8X4),
                scales=scales[:, lo:hi],
                in_=woven[which, b][:, lo:hi, :].rearrange("p c t -> p (c t)"),
            )

        def weave_and_quantise_group0(which):
            weave(nc.scalar.copy, which, 0, 0, NP // 2)
            weave(nc.scalar.copy, which, 0, NP // 2, NP)
            quantise_x(which, 0, 0, NP)

        sums_e = []

        def score_pass(u, b):
            if b == 0:
                sums_e.append(psum.tile([P, NP], F32, name="sum_e", tag="b"))
            nc.tensor.matmul_mx(
                out=sums_e[u][:],
                lhsT=x_quantised[1, b][0][:, P * u : P * (u + 1)].bitcast(FP8X4),
                lhsT_scale=x_quantised[1, b][1][:, P * u : P * (u + 1)],
                rhs=x_quantised[2, b][0][:].bitcast(FP8X4),
                rhs_scale=x_quantised[2, b][1][:],
                start=(b == 0),
                stop=(b == GROUPS - 1),
            )

        def finish(u):
            score_pass(u, 1)
            weighted = ring.tile([P, NP], F32, name="weighted", bufs=NP // P)
            nc.vector.tensor_tensor(weighted[:], sums_e[u][:], client_t[:, u, :], ALU.mult)
            scored = ring.tile([P, NP], F32, name="scored", bufs=NP // P)
            nc.scalar.activation(scored[:], weighted[:], ACT.Identity, bias=d_t[:, u : u + 1])
            nc.sync.dma_start(out[P * u : P * (u + 1), :], scored[:])

        fraction_of_turn(0)
        sine(0)
        round_w1(0)
        quantise_w1(0)
        for n in range(-1, TILES + 1):
            ahead = n + 2
            if ahead < TILES_COUNTED_BY_VECTOR:
                fraction_of_turn(ahead)
                round_w1(ahead)
                quantise_w1(ahead)
            elif ahead < TILES:
                round_w1(ahead)
                fraction_of_turn(ahead)
                quantise_w1(ahead)
            if 1 <= n + 1 < TILES:
                sine(n + 1)
            if 0 <= n < TILES:
                rows_of_h(n)
            if 0 <= n - 1:
                magnitude(n - 1)
            if n == TILES - 2:
                weave_and_quantise_group0(2)
            if n == TILES - 1:
                weave_and_quantise_group0(1)
                for u in range(NP // P):
                    score_pass(u, 0)

        weave(nc.vector.tensor_copy, 2, 1, 0, NP)
        quantise_x(2, 1, 0, NP)
        for lo in range(0, NP, NP // 2):
            hi = lo + NP // 2
            weave(nc.scalar.copy, 1, 1, lo, hi)
            quantise_x(1, 1, lo, hi)
            for u in range(lo // P, hi // P):
                finish(u)
